import numpy as np
CORES = [88,89,90,91,92,93,94,95,96,97,98,99,100,101,102,103]
N = 16
def setup_inputs(rng):
    return {"x": rng.standard_normal((N, 128, 16), dtype=np.float32)}
def reference(x):
    s = x.max(axis=0)
    b = 16 // N
    return {"y": np.stack([s[:, r * b:(r + 1) * b] for r in range(N)])}

@@ -1,0 +1,68 @@
+from concourse.bass import DstId, RemoteDMATransfer
+
+SCRATCH = {
+    "xs": ("sbuf", [128, 16], "float32"),
+    "land": ("sbuf", [128, 16], "float32"),
+    "part": ("sbuf", [128, 2], "float32"),
+    "res": ("sbuf", [128, 1], "float32"),
+}
+SEMAPHORES = ["loaded", "gath", "cross", "fin", "sent", "stored"]
+
+HOME = [5, 0, 1, 4]
+AWAY = [7, 2, 3, 6]
+MAX = 2
+
+
+def rank_program(g, core, T, topo):
+    rank = T.rank_of(core)
+    if rank is None:
+        return
+    side, k = divmod(rank, 8)
+    base = T.cores[8 * side]
+    other = T.cores[8 * (1 - side)]
+
+    def did(c):
+        rid, pid, _se = topo.addr(c)
+        return DstId(rid=rid, pnc=pid)
+
+    def pair_of(kk):
+        if kk in HOME:
+            return 4 * side + HOME.index(kk)
+        return 4 * (1 - side) + AWAY.index(kk)
+
+    g.dma_start(T.xs[:], T.x[:]).then_inc(T.sem.loaded, 16)
+    g.wait_ge(T.sem.loaded, 16)
+
+    trs = []
+    for i, kk in enumerate([j for j in range(8) if j != k]):
+        b = pair_of(kk)
+        trs.append(RemoteDMATransfer(dst_ids=[did(base + kk)], dma_engine_mask=0b11 << (2 * i),
+                                     remote_sem=T.sem.gath,
+                                     src=T.xs[:, 2 * b:2 * b + 2], dst=T.land[:, 2 * k:2 * k + 2]))
+    g.remote_dma_fused(trs, local_sem=T.sem.sent)
+    sent = 14
+
+    g.wait_ge(T.sem.gath, 14)
+    b = pair_of(k)
+    if k in AWAY:
+        srcs = [T.land[:, 2 * j:2 * j + 2] for j in range(8) if j != k] + [T.xs[:, 2 * b:2 * b + 2]]
+        dst = other + HOME[AWAY.index(k)]
+        g.remote_dma_fused([RemoteDMATransfer(dst_ids=[did(dst)], dma_engine_mask=0x00FF, remote_sem=T.sem.cross,
+                                              srcs=srcs, dsts=[T.part[:]], alu_op=MAX)], local_sem=T.sem.sent)
+        sent += 8
+    else:
+        g.wait_ge(T.sem.cross, 8)
+        t = HOME.index(k)
+        trs = []
+        for c in range(2):
+            srcs = [T.land[:, 2 * j + c:2 * j + c + 1] for j in range(8) if j != k]
+            srcs += [T.xs[:, 2 * b + c:2 * b + c + 1], T.part[:, c:c + 1]]
+            trs.append(RemoteDMATransfer(dst_ids=[did(base + 2 * t + c)], dma_engine_mask=0xFF << (8 * c),
+                                         remote_sem=T.sem.fin, srcs=srcs, dsts=[T.res[:]], alu_op=MAX))
+        g.remote_dma_fused(trs, local_sem=T.sem.sent)
+        sent += 16
+
+    g.wait_ge(T.sem.fin, 8)
+    g.dma_start(T.y[:], T.res[:]).then_inc(T.sem.stored, 16)
+    g.wait_ge(T.sem.stored, 16)
+    g.wait_ge(T.sem.sent, sent)

@@ -1,15 +1,12 @@
 from concourse.bass import DstId, RemoteDMATransfer
 
 SCRATCH = {
-    "xs": ("sbuf", [128, 16], "float32"),
-    "land": ("sbuf", [128, 16], "float32"),
-    "part": ("sbuf", [128, 2], "float32"),
-    "res": ("sbuf", [128, 1], "float32"),
+    "stage": ("dram", [8, 128, 2], "float32"),
+    "land": ("dram", [8, 128, 2], "float32"),
+    "part": ("dram", [128, 2], "float32"),
+    "fin": ("dram", [256, 2], "float32"),
 }
 SEMAPHORES = ["loaded", "gath", "cross", "fin", "sent", "stored"]
-
-HOME = [5, 0, 1, 4]
-AWAY = [7, 2, 3, 6]
 MAX = 2
 
 
@@ -25,44 +22,42 @@ def rank_program(g, core, T, topo):
         rid, pid, _se = topo.addr(c)
         return DstId(rid=rid, pnc=pid)
 
-    def pair_of(kk):
-        if kk in HOME:
-            return 4 * side + HOME.index(kk)
-        return 4 * (1 - side) + AWAY.index(kk)
+    def piece_of(kk):
+        owner_side = side if kk % 4 < 2 else 1 - side
+        low_or_high = 1 if kk < 4 else 0
+        return 2 * (2 * owner_side + low_or_high) + kk % 2
 
-    g.dma_start(T.xs[:], T.x[:]).then_inc(T.sem.loaded, 16)
-    g.wait_ge(T.sem.loaded, 16)
+    for q in range(4):
+        queue = g.sync if q % 2 == 0 else g.scalar
+        queue.dma_start(T.stage[2 * q:2 * q + 2], T.x[:, 4 * q:4 * q + 4]).then_inc(T.sem.loaded, 16)
+    g.wait_ge(T.sem.loaded, 64)
 
     trs = []
     for i, kk in enumerate([j for j in range(8) if j != k]):
-        b = pair_of(kk)
         trs.append(RemoteDMATransfer(dst_ids=[did(base + kk)], dma_engine_mask=0b11 << (2 * i),
-                                     remote_sem=T.sem.gath,
-                                     src=T.xs[:, 2 * b:2 * b + 2], dst=T.land[:, 2 * k:2 * k + 2]))
+                                     remote_sem=T.sem.gath, src=T.stage[piece_of(kk)], dst=T.land[k]))
     g.remote_dma_fused(trs, local_sem=T.sem.sent)
     sent = 14
 
     g.wait_ge(T.sem.gath, 14)
-    b = pair_of(k)
-    if k in AWAY:
-        srcs = [T.land[:, 2 * j:2 * j + 2] for j in range(8) if j != k] + [T.xs[:, 2 * b:2 * b + 2]]
-        dst = other + HOME[AWAY.index(k)]
-        g.remote_dma_fused([RemoteDMATransfer(dst_ids=[did(dst)], dma_engine_mask=0x00FF, remote_sem=T.sem.cross,
-                                              srcs=srcs, dsts=[T.part[:]], alu_op=MAX)], local_sem=T.sem.sent)
+    srcs = [T.land[j] for j in range(8) if j != k] + [T.stage[piece_of(k)]]
+    if k % 4 >= 2:
+        g.remote_dma_fused([RemoteDMATransfer(dst_ids=[did(other + k - 2)], dma_engine_mask=0x00FF,
+                                              remote_sem=T.sem.cross, srcs=srcs, dsts=[T.part[:]], alu_op=MAX)],
+                           local_sem=T.sem.sent)
         sent += 8
     else:
         g.wait_ge(T.sem.cross, 8)
-        t = HOME.index(k)
-        trs = []
-        for c in range(2):
-            srcs = [T.land[:, 2 * j + c:2 * j + c + 1] for j in range(8) if j != k]
-            srcs += [T.xs[:, 2 * b + c:2 * b + c + 1], T.part[:, c:c + 1]]
-            trs.append(RemoteDMATransfer(dst_ids=[did(base + 2 * t + c)], dma_engine_mask=0xFF << (8 * c),
-                                         remote_sem=T.sem.fin, srcs=srcs, dsts=[T.res[:]], alu_op=MAX))
-        g.remote_dma_fused(trs, local_sem=T.sem.sent)
+        h = k % 2
+        owners = [base + (4 if k < 4 else 0) + j for j in range(4)]
+        g.remote_dma_fused([RemoteDMATransfer(dst_ids=[did(o) for o in owners], dma_engine_mask=0xFFFF,
+                                              remote_sem=T.sem.fin, srcs=srcs + [T.part[:]],
+                                              dsts=[T.fin[128 * h:128 * h + 128, :] for _o in owners], alu_op=MAX)],
+                           local_sem=T.sem.sent)
         sent += 16
 
-    g.wait_ge(T.sem.fin, 8)
-    g.dma_start(T.y[:], T.res[:]).then_inc(T.sem.stored, 16)
+    g.wait_ge(T.sem.fin, 32)
+    c = k % 4
+    g.dma_start(T.y[:], T.fin[c // 2::2, c % 2:c % 2 + 1], allow_slow_non_contiguous=True).then_inc(T.sem.stored, 16)
     g.wait_ge(T.sem.stored, 16)
     g.wait_ge(T.sem.sent, sent)

from concourse.bass import DstId, RemoteDMATransfer

SCRATCH = {
    "stage": ("dram", [8, 128, 2], "float32"),
    "land": ("dram", [8, 128, 2], "float32"),
    "part": ("dram", [128, 2], "float32"),
    "fin": ("dram", [256, 2], "float32"),
}
SEMAPHORES = ["loaded", "gath", "cross", "fin", "sent", "stored"]
MAX = 2


def rank_program(g, core, T, topo):
    rank = T.rank_of(core)
    if rank is None:
        return
    side, k = divmod(rank, 8)
    base = T.cores[8 * side]
    other = T.cores[8 * (1 - side)]

    def did(c):
        rid, pid, _se = topo.addr(c)
        return DstId(rid=rid, pnc=pid)

    def piece_of(kk):
        owner_side = side if kk % 4 < 2 else 1 - side
        low_or_high = 1 if kk < 4 else 0
        return 2 * (2 * owner_side + low_or_high) + kk % 2

    for q in range(4):
        queue = g.sync if q % 2 == 0 else g.scalar
        queue.dma_start(T.stage[2 * q:2 * q + 2], T.x[:, 4 * q:4 * q + 4]).then_inc(T.sem.loaded, 16)
    g.wait_ge(T.sem.loaded, 64)

    trs = []
    for i, kk in enumerate([j for j in range(8) if j != k]):
        trs.append(RemoteDMATransfer(dst_ids=[did(base + kk)], dma_engine_mask=0b11 << (2 * i),
                                     remote_sem=T.sem.gath, src=T.stage[piece_of(kk)], dst=T.land[k]))
    g.remote_dma_fused(trs, local_sem=T.sem.sent)
    sent = 14

    g.wait_ge(T.sem.gath, 14)
    srcs = [T.land[j] for j in range(8) if j != k] + [T.stage[piece_of(k)]]
    if k % 4 >= 2:
        g.remote_dma_fused([RemoteDMATransfer(dst_ids=[did(other + k - 2)], dma_engine_mask=0x00FF,
                                              remote_sem=T.sem.cross, srcs=srcs, dsts=[T.part[:]], alu_op=MAX)],
                           local_sem=T.sem.sent)
        sent += 8
    else:
        g.wait_ge(T.sem.cross, 8)
        h = k % 2
        owners = [base + (4 if k < 4 else 0) + j for j in range(4)]
        g.remote_dma_fused([RemoteDMATransfer(dst_ids=[did(o) for o in owners], dma_engine_mask=0xFFFF,
                                              remote_sem=T.sem.fin, srcs=srcs + [T.part[:]],
                                              dsts=[T.fin[128 * h:128 * h + 128, :] for _o in owners], alu_op=MAX)],
                           local_sem=T.sem.sent)
        sent += 16

    g.wait_ge(T.sem.fin, 32)
    c = k % 4
    g.dma_start(T.y[:], T.fin[c // 2::2, c % 2:c % 2 + 1], allow_slow_non_contiguous=True).then_inc(T.sem.stored, 16)
    g.wait_ge(T.sem.stored, 16)
    g.wait_ge(T.sem.sent, sent)
